import numpy as np
import ml_dtypes


def mxq(x, axis, fmt="e4m3"):
    dtype, down = {"e4m3": (ml_dtypes.float8_e4m3fn, 7), "e5m2": (ml_dtypes.float8_e5m2, 14)}[fmt]
    v = np.moveaxis(np.asarray(x, np.float32).astype(ml_dtypes.bfloat16).astype(np.float64), axis, -1)
    blocks = v.reshape(v.shape[:-1] + (-1, 32))
    amax = np.abs(blocks).max(-1, keepdims=True)
    byte = np.maximum(np.where(amax > 0, np.frexp(amax)[1] - 1 + 127, 0) - down, 1)
    scale = np.exp2(byte - 127.0)
    codes = (blocks / scale).astype(np.float32).astype(dtype).astype(np.float64)
    return np.moveaxis((codes * scale).reshape(v.shape), -1, axis)


WIDE = False


def mx_kscale(k):
    if not WIDE:
        return np.ones(k)
    levels = np.array([10, -10, 5, -5, 0])
    if k % 512:
        return np.exp2(np.random.permutation(np.resize(levels, k // 32))).repeat(32)
    a = np.empty((k // 512, 16))
    for p in range(k // 512):
        a[p, :8] = np.random.permutation(np.resize(levels, 8))
        for g in range(8):
            far = levels[np.abs(levels - a[p, g]) >= 10]
            a[p, g + 8] = far[np.random.randint(len(far))]
    return np.exp2(a.ravel()).repeat(32)


def f64(x):
    return np.asarray(x).astype(np.float64)


def striped(idx):
    return np.tile(idx.reshape(-1, 16).T, (8, 1)).astype(np.uint16)


def unstriped(offs):
    return offs[:16].T.reshape(-1).astype(np.int64)


E2M1 = np.array([0.0, 0.5, 1.0, 1.5, 2.0, 3.0, 4.0, 6.0, -0.0, -0.5, -1.0, -1.5, -2.0, -3.0, -4.0, -6.0])


def pack_weight(w, fmt):
    k, n = w.shape
    w = f64(np.asarray(w, np.float32).astype(ml_dtypes.bfloat16)).reshape(k // 32, 32, n)
    amax = np.abs(w).max(1)
    if fmt == "e4m3":
        byte = np.frexp(amax)[1] - 1 + 127 - 7
    else:
        mant, ex = np.frexp(amax / 6.0)
        byte = np.where(mant > 0.5, ex, ex - 1) + 127
    byte = np.clip(np.where(amax > 0, byte, 1), 1, 254)
    scaled = (w * np.exp2(127.0 - byte)[:, None, :]).reshape(k, n).astype(np.float32)
    by_word = np.ascontiguousarray(scaled.reshape(k // 512, 128, 4, n).transpose(0, 1, 3, 2))
    if fmt == "e4m3":
        words = by_word.astype(ml_dtypes.float8_e4m3fn).view(np.uint8)
    else:
        c = by_word.astype(ml_dtypes.float4_e2m1fn).view(np.uint8) & 0xF
        words = (c[..., 0::2] | (c[..., 1::2] << 4)).reshape(k // 512, 128, 2 * n)
    return np.ascontiguousarray(words), np.ascontiguousarray(byte.astype(np.uint8).reshape(k // 512, 16, n))


def unpack_weight(words, scales, fmt):
    g, _, n = scales.shape
    words = np.ascontiguousarray(words).reshape(g, 128, n, -1)
    if fmt == "e4m3":
        vals = words.view(ml_dtypes.float8_e4m3fn).astype(np.float64)
    else:
        nib = np.empty((g, 128, n, 4), np.uint8)
        nib[..., 0::2] = words & 0xF
        nib[..., 1::2] = words >> 4
        vals = E2M1[nib]
    vals = vals * np.repeat(np.exp2(scales.astype(np.float64) - 127.0), 8, axis=1)[..., None]
    return vals.transpose(0, 1, 3, 2).reshape(g * 512, n)


def relu2(v):
    return np.maximum(v, 0.0) ** 2


K, T, E, C, H, N = 512, 512, 2, 256, 512, 512


def by_expert(wq, xq):
    return np.concatenate([wq[e].T @ xq[:, e * C:(e + 1) * C] for e in range(E)], axis=1)


def setup_inputs():
    n = np.random.standard_normal
    s = mx_kscale(K)[:, None]
    u = mx_kscale(H)
    w1 = [pack_weight(m, "e2m1") for m in n((E, K, H)) / np.sqrt(K) / s[None] * u[None, None, :]]
    w2 = [pack_weight(m, "e2m1") for m in n((E, H, N)) / np.sqrt(H) / u[None, :, None] ** 2]
    return {
        "xT": (n((K, T)) * s).astype(np.float32),
        "w1_words": np.stack([m[0] for m in w1]),
        "w1_scales": np.stack([m[1] for m in w1]),
        "w2_words": np.stack([m[0] for m in w2]),
        "w2_scales": np.stack([m[1] for m in w2]),
        "gate": np.tile(np.random.uniform(0.2, 1.0, E * C), (N, 1)).astype(np.float32),
        "offs": striped(np.random.permutation(T)[:E * C]),
        "dst": striped(np.random.permutation(T)[:E * C]),
    }


def reference(xT, w1_words, w1_scales, w2_words, w2_scales, gate, offs, dst):
    idx = unstriped(offs)
    w1 = np.stack([unpack_weight(w1_words[e], w1_scales[e], "e2m1") for e in range(E)])
    w2 = np.stack([unpack_weight(w2_words[e], w2_scales[e], "e2m1") for e in range(E)])
    xq = mxq(f64(xT)[:, idx], 0, "e4m3")
    h = relu2(by_expert(w1, xq))
    y = by_expert(w2, mxq(h, 0, "e4m3"))
    out = np.zeros((N, T))
    out[:, unstriped(dst)] = f64(gate) * y
    return out

@@ -1,0 +1,160 @@
+from contextlib import ExitStack
+
+import concourse.mybir as mybir
+
+F32 = mybir.dt.float32
+BF16 = mybir.dt.bfloat16
+I32 = mybir.dt.int32
+U32 = mybir.dt.uint32
+U16 = mybir.dt.uint16
+U8 = mybir.dt.uint8
+FP8X4 = mybir.dt.float8_e4m3fn_x4
+FP4X4 = mybir.dt.float4_e2m1fn_x4
+MULT = mybir.AluOpType.mult
+RELU = mybir.ActivationFunctionType.Relu
+SQUARE = mybir.ActivationFunctionType.Square
+
+P = 128
+K, T, E, C, H, N = 512, 512, 2, 256, 512, 512
+CHUNK = 128
+FLOPS = 2 * E * C * H * (K + N)
+
+
+def tile_moe_two_mlp_relu2_kernel(tc, xT, w1_words, w1_scales, w2_words, w2_scales, gate, offs, dst, out):
+    nc = tc.nc
+    with ExitStack() as ctx:
+        keep = ctx.enter_context(tc.tile_pool(name="keep", bufs=1))
+        psum = ctx.enter_context(tc.psum_pool(name="psum", bufs=1))
+
+        offs_t = keep.tile([P, T // 16], U16, name="offs_t")
+        dst_t = keep.tile([P, T // 16], U16, name="dst_t")
+        s1_raw = keep.tile([P, E, H], U8, name="s1_raw", align_bytes=64)
+        s2 = keep.tile([P, E, N], U8, name="s2", align_bytes=64)
+        xs = keep.tile([P, T], U8, name="xs", align_bytes=64)
+        xw = keep.tile([P, T], U32, name="xw", align_bytes=64)
+        warm = keep.tile([P, 1], F32, name="warm")
+
+        nc.gpsimd.memset(xs[:], 0)
+        nc.vector.memset(s1_raw[:].rearrange("p e i -> p (e i)").bitcast(I32), 0)
+        nc.vector.memset(s2[:].rearrange("p e i -> p (e i)").bitcast(I32), 0)
+        nc.vector.memset(warm[:], 0.0)
+        nc.scalar.activation(warm[:], warm[:], SQUARE)
+
+        w1_raw = [keep.tile([P, 2 * H], U8, name=f"w1_raw{e}", align_bytes=64) for e in range(E)]
+        w2 = [keep.tile([P, 2 * N], U8, name=f"w2_{e}", align_bytes=64) for e in range(E)]
+
+        nc.sync.dma_start(offs_t[:], offs)
+        x_rows = xT.rearrange("(p j) w -> p j w", j=4)
+        x_raw = [keep.tile([P, 4, CHUNK], F32, name=f"x_raw{c}", align_bytes=64) for c in range(T // CHUNK)]
+        for c in range(T // CHUNK):
+            nc.sync.dma_start(x_raw[c][:], x_rows[:, :, c * CHUNK : (c + 1) * CHUNK])
+            if c == 1:
+                nc.sync.dma_start(w1_raw[0][:].bitcast(I32), w1_words[0, 0].bitcast(I32))
+        nc.sync.dma_start(w1_raw[1][:].bitcast(I32), w1_words[1, 0].bitcast(I32))
+        for q in range(4):
+            nc.scalar.dma_start(
+                s1_raw[32 * q : 32 * q + 4].bitcast(I32),
+                w1_scales[:, 0, 4 * q : 4 * q + 4, :].rearrange("e q i -> q e i").bitcast(I32),
+            )
+        for q in range(4):
+            nc.scalar.dma_start(
+                s2[32 * q : 32 * q + 4].bitcast(I32),
+                w2_scales[:, 0, 4 * q : 4 * q + 4, :].rearrange("e q i -> q e i").bitcast(I32),
+            )
+        gate_t = keep.tile([P, E * C], F32, name="gate_t")
+        nc.sync.dma_start(w2[0][:].bitcast(I32), w2_words[0, 0].bitcast(I32))
+        nc.sync.dma_start(gate_t[:], gate[0:P, :])
+        nc.sync.dma_start(dst_t[:], dst)
+        nc.sync.dma_start(w2[1][:].bitcast(I32), w2_words[1, 0].bitcast(I32))
+
+        w1 = [keep.tile([P, 2 * H], U8, name=f"w1_{e}", align_bytes=64) for e in range(E)]
+        s1 = [keep.tile([P, H], U8, name=f"s1_{e}", align_bytes=64) for e in range(E)]
+
+        def permute(e):
+            nc.vector.tensor_copy(
+                w1[e][:].bitcast(U16).rearrange("p (t m) -> p t m", t=4),
+                w1_raw[e][:].bitcast(U16).rearrange("p (m t) -> p t m", t=4),
+            )
+            nc.vector.tensor_copy(
+                s1[e][:].rearrange("p (t m) -> p t m", t=4),
+                s1_raw[:, e, :].rearrange("p (m t) -> p t m", t=4),
+            )
+
+        permute(0)
+
+        x_grp = [keep.tile([P, CHUNK, 4], BF16, name=f"x_grp{c}", align_bytes=64) for c in range(T // CHUNK)]
+        for c in range(T // CHUNK):
+            src = x_raw[c][:].rearrange("p j w -> p w j")
+            if c % 2 == 0:
+                nc.scalar.copy(x_grp[c][:], src)
+            else:
+                nc.vector.tensor_copy(x_grp[c][:], src)
+            cols = slice(c * CHUNK, (c + 1) * CHUNK)
+            nc.vector.quantize_mx(
+                out=xw[:, cols].bitcast(FP8X4), scales=xs[:, cols], in_=x_grp[c][:].rearrange("p w j -> p (w j)")
+            )
+
+        gw = [keep.tile([P, C], U32, name=f"gw{e}", align_bytes=64) for e in range(E)]
+        gs = [keep.tile([P, C], U8, name=f"gs{e}", align_bytes=64) for e in range(E)]
+        a_ps = [[psum.tile([P, 2, C], F32, name=f"a_ps{e}_{b}") for b in range(2)] for e in range(E)]
+        y_ps = [[psum.tile([P, 2, C], F32, name=f"y_ps{e}_{b}") for b in range(2)] for e in range(E)]
+        r = [keep.tile([P, 4, C], F32, name=f"r{e}", align_bytes=64) for e in range(E)]
+        h_grp = [keep.tile([P, C, 4], BF16, name=f"h_grp{e}", align_bytes=64) for e in range(E)]
+        hw = [keep.tile([P, C], U32, name=f"hw{e}", align_bytes=64) for e in range(E)]
+        hs = [keep.tile([P, C], U8, name=f"hs{e}", align_bytes=64) for e in range(E)]
+        y_sb = [[keep.tile([P, 2, C], F32, name=f"y_sb{e}_{b}") for b in range(2)] for e in range(E)]
+        win = [keep.tile([P, T], F32, name=f"win{b}") for b in range(4)]
+
+        for e in range(E):
+            lst = offs_t[:, e * (C // 16) : (e + 1) * (C // 16)]
+            nc.vector.tensor_copy(gw[e][:], xw[:].indirect(lst))
+            nc.vector.tensor_copy(gs[e][:], xs[:].indirect(lst))
+            if e == 1:
+                permute(1)
+            for t in range(4):
+                nc.tensor.matmul_mx(
+                    out=a_ps[e][t // 2][:, t % 2, :],
+                    lhsT=w1[e][:, 256 * t : 256 * (t + 1)].bitcast(FP4X4),
+                    lhsT_scale=s1[e][:, P * t : P * (t + 1)],
+                    rhs=gw[e][:].bitcast(FP8X4),
+                    rhs_scale=gs[e][:],
+                    start=True,
+                    stop=True,
+                )
+        for e in range(E):
+            for b in range(2):
+                nc.scalar.activation(r[e][:, 2 * b : 2 * b + 2, :], a_ps[e][b][:], RELU)
+            half = C // 2
+            for s in range(2):
+                cols = slice(s * half, (s + 1) * half)
+                src = r[e][:, :, cols].rearrange("p t s -> p s t")
+                if e == 0 and s == 1:
+                    nc.vector.tensor_tensor(h_grp[e][:, cols, :], src, src, MULT)
+                else:
+                    nc.scalar.activation(h_grp[e][:, cols, :], src, SQUARE)
+            nc.vector.quantize_mx(
+                out=hw[e][:].bitcast(FP8X4), scales=hs[e][:], in_=h_grp[e][:].rearrange("p s t -> p (s t)")
+            )
+            for b in range(4):
+                nc.tensor.matmul_mx(
+                    out=y_ps[e][b // 2][:, b % 2, :],
+                    lhsT=w2[e][:, 256 * b : 256 * (b + 1)].bitcast(FP4X4),
+                    lhsT_scale=s2[:, e, P * b : P * (b + 1)],
+                    rhs=hw[e][:].bitcast(FP8X4),
+                    rhs_scale=hs[e][:],
+                    start=True,
+                    stop=True,
+                )
+            for b in range(4):
+                if b % 2 == 0:
+                    nc.vector.tensor_tensor(
+                        y_sb[e][b // 2][:],
+                        y_ps[e][b // 2][:],
+                        gate_t[:, e * C : (e + 1) * C].unsqueeze(1).to_broadcast([P, 2, C]),
+                        MULT,
+                    )
+                nc.vector.tensor_copy(
+                    win[b][:].indirect(dst_t[:, e * (C // 16) : (e + 1) * (C // 16)]), y_sb[e][b // 2][:, b % 2, :]
+                )
+                if e == E - 1:
+                    nc.sync.dma_start(out[b * P : (b + 1) * P, :], win[b][:])

@@ -16,7 +16,8 @@ SQUARE = mybir.ActivationFunctionType.Square
 
 P = 128
 K, T, E, C, H, N = 512, 512, 2, 256, 512, 512
-CHUNK = 128
+X0 = 384
+UNITS = ((0, 0, 128), (0, 128, 256), (1, 0, 256))
 FLOPS = 2 * E * C * H * (K + N)
 
 
@@ -33,128 +34,170 @@ def tile_moe_two_mlp_relu2_kernel(tc, xT, w1_words, w1_scales, w2_words, w2_scal
         xs = keep.tile([P, T], U8, name="xs", align_bytes=64)
         xw = keep.tile([P, T], U32, name="xw", align_bytes=64)
         warm = keep.tile([P, 1], F32, name="warm")
+        w1_raw = keep.tile([P, E, 2 * H], U8, name="w1_raw", align_bytes=64)
+        w2 = keep.tile([P, E, 2 * N], U8, name="w2", align_bytes=64)
+        x_raw = [keep.tile([P, 4, w], F32, name=f"x_raw{w}", align_bytes=64) for w in (X0, T - X0)]
+        gate_t = keep.tile([P, E * C], F32, name="gate_t")
 
-        nc.gpsimd.memset(xs[:], 0)
         nc.vector.memset(s1_raw[:].rearrange("p e i -> p (e i)").bitcast(I32), 0)
+        nc.gpsimd.memset(xs[:], 0)
         nc.vector.memset(s2[:].rearrange("p e i -> p (e i)").bitcast(I32), 0)
         nc.vector.memset(warm[:], 0.0)
         nc.scalar.activation(warm[:], warm[:], SQUARE)
 
-        w1_raw = [keep.tile([P, 2 * H], U8, name=f"w1_raw{e}", align_bytes=64) for e in range(E)]
-        w2 = [keep.tile([P, 2 * N], U8, name=f"w2_{e}", align_bytes=64) for e in range(E)]
-
-        nc.sync.dma_start(offs_t[:], offs)
         x_rows = xT.rearrange("(p j) w -> p j w", j=4)
-        x_raw = [keep.tile([P, 4, CHUNK], F32, name=f"x_raw{c}", align_bytes=64) for c in range(T // CHUNK)]
-        for c in range(T // CHUNK):
-            nc.sync.dma_start(x_raw[c][:], x_rows[:, :, c * CHUNK : (c + 1) * CHUNK])
-            if c == 1:
-                nc.sync.dma_start(w1_raw[0][:].bitcast(I32), w1_words[0, 0].bitcast(I32))
-        nc.sync.dma_start(w1_raw[1][:].bitcast(I32), w1_words[1, 0].bitcast(I32))
+        nc.sync.dma_start(offs_t[:], offs)
+        nc.sync.dma_start(w1_raw[:].bitcast(I32), w1_words[:, 0].rearrange("e p b -> p e b").bitcast(I32))
+        nc.sync.dma_start(x_raw[0][:], x_rows[:, :, 0:X0])
+        nc.sync.dma_start(x_raw[1][:], x_rows[:, :, X0:T])
         for q in range(4):
             nc.scalar.dma_start(
                 s1_raw[32 * q : 32 * q + 4].bitcast(I32),
                 w1_scales[:, 0, 4 * q : 4 * q + 4, :].rearrange("e q i -> q e i").bitcast(I32),
             )
+        nc.sync.dma_start(w2[:].bitcast(I32), w2_words[:, 0].rearrange("e p b -> p e b").bitcast(I32))
+        nc.sync.dma_start(dst_t[:], dst)
+        nc.sync.dma_start(gate_t[:], gate[0:P, :])
         for q in range(4):
-            nc.scalar.dma_start(
+            nc.gpsimd.dma_start(
                 s2[32 * q : 32 * q + 4].bitcast(I32),
                 w2_scales[:, 0, 4 * q : 4 * q + 4, :].rearrange("e q i -> q e i").bitcast(I32),
             )
-        gate_t = keep.tile([P, E * C], F32, name="gate_t")
-        nc.sync.dma_start(w2[0][:].bitcast(I32), w2_words[0, 0].bitcast(I32))
-        nc.sync.dma_start(gate_t[:], gate[0:P, :])
-        nc.sync.dma_start(dst_t[:], dst)
-        nc.sync.dma_start(w2[1][:].bitcast(I32), w2_words[1, 0].bitcast(I32))
 
-        w1 = [keep.tile([P, 2 * H], U8, name=f"w1_{e}", align_bytes=64) for e in range(E)]
-        s1 = [keep.tile([P, H], U8, name=f"s1_{e}", align_bytes=64) for e in range(E)]
+        w1 = keep.tile([P, E, 2 * H], U8, name="w1", align_bytes=64)
+        s1 = keep.tile([P, E, H], U8, name="s1", align_bytes=64)
 
         def permute(e):
             nc.vector.tensor_copy(
-                w1[e][:].bitcast(U16).rearrange("p (t m) -> p t m", t=4),
-                w1_raw[e][:].bitcast(U16).rearrange("p (m t) -> p t m", t=4),
+                w1[:, e, :].bitcast(U16).rearrange("p (t m) -> p t m", t=4),
+                w1_raw[:, e, :].bitcast(U16).rearrange("p (m t) -> p t m", t=4),
             )
             nc.vector.tensor_copy(
-                s1[e][:].rearrange("p (t m) -> p t m", t=4),
+                s1[:, e, :].rearrange("p (t m) -> p t m", t=4),
                 s1_raw[:, e, :].rearrange("p (m t) -> p t m", t=4),
             )
 
         permute(0)
 
-        x_grp = [keep.tile([P, CHUNK, 4], BF16, name=f"x_grp{c}", align_bytes=64) for c in range(T // CHUNK)]
-        for c in range(T // CHUNK):
-            src = x_raw[c][:].rearrange("p j w -> p w j")
-            if c % 2 == 0:
-                nc.scalar.copy(x_grp[c][:], src)
+        x_grp = [keep.tile([P, w, 4], BF16, name=f"x_grp{w}", align_bytes=64) for w in (X0, T - X0)]
+
+        def group(i, a, b, engine):
+            src = x_raw[i][:, :, a:b].rearrange("p j w -> p w j")
+            if engine == "s":
+                nc.scalar.copy(x_grp[i][:, a:b, :], src)
             else:
-                nc.vector.tensor_copy(x_grp[c][:], src)
-            cols = slice(c * CHUNK, (c + 1) * CHUNK)
+                nc.vector.tensor_copy(x_grp[i][:, a:b, :], src)
+
+        def quantize_x(i, a, b):
+            cols = slice(i * X0 + a, i * X0 + b)
             nc.vector.quantize_mx(
-                out=xw[:, cols].bitcast(FP8X4), scales=xs[:, cols], in_=x_grp[c][:].rearrange("p w j -> p (w j)")
+                out=xw[:, cols].bitcast(FP8X4),
+                scales=xs[:, cols],
+                in_=x_grp[i][:, a:b, :].rearrange("p w j -> p (w j)"),
             )
+
+        group(0, 0, 256, "s")
+        group(0, 256, 384, "v")
+        quantize_x(0, 256, 384)
+        group(1, 0, 64, "s")
+        group(1, 64, 128, "v")
+        quantize_x(0, 0, 256)
+        quantize_x(1, 0, 128)
 
         gw = [keep.tile([P, C], U32, name=f"gw{e}", align_bytes=64) for e in range(E)]
         gs = [keep.tile([P, C], U8, name=f"gs{e}", align_bytes=64) for e in range(E)]
-        a_ps = [[psum.tile([P, 2, C], F32, name=f"a_ps{e}_{b}") for b in range(2)] for e in range(E)]
-        y_ps = [[psum.tile([P, 2, C], F32, name=f"y_ps{e}_{b}") for b in range(2)] for e in range(E)]
-        r = [keep.tile([P, 4, C], F32, name=f"r{e}", align_bytes=64) for e in range(E)]
-        h_grp = [keep.tile([P, C, 4], BF16, name=f"h_grp{e}", align_bytes=64) for e in range(E)]
-        hw = [keep.tile([P, C], U32, name=f"hw{e}", align_bytes=64) for e in range(E)]
-        hs = [keep.tile([P, C], U8, name=f"hs{e}", align_bytes=64) for e in range(E)]
-        y_sb = [[keep.tile([P, 2, C], F32, name=f"y_sb{e}_{b}") for b in range(2)] for e in range(E)]
+        a_ps, y_ps, r, h_grp, hw, hs, y_sb = [], [], [], [], [], [], []
+        for u, (e, a, b) in enumerate(UNITS):
+            w = b - a
+            a_ps.append([psum.tile([P, 512 // w, w], F32, name=f"a_ps{u}_{i}") for i in range(4 * w // 512)])
+            y_ps.append([psum.tile([P, 512 // w, w], F32, name=f"y_ps{u}_{i}") for i in range(4 * w // 512)])
+            r.append(keep.tile([P, 4, w], F32, name=f"r{u}", align_bytes=64))
+            h_grp.append(keep.tile([P, w, 4], BF16, name=f"h_grp{u}", align_bytes=64))
+            hw.append(keep.tile([P, w], U32, name=f"hw{u}", align_bytes=64))
+            hs.append(keep.tile([P, w], U8, name=f"hs{u}", align_bytes=64))
+            y_sb.append(keep.tile([P, 4, w], F32, name=f"y_sb{u}"))
         win = [keep.tile([P, T], F32, name=f"win{b}") for b in range(4)]
 
-        for e in range(E):
-            lst = offs_t[:, e * (C // 16) : (e + 1) * (C // 16)]
-            nc.vector.tensor_copy(gw[e][:], xw[:].indirect(lst))
-            nc.vector.tensor_copy(gs[e][:], xs[:].indirect(lst))
-            if e == 1:
-                permute(1)
+        def gather(u):
+            e, a, b = UNITS[u]
+            lst = offs_t[:, (e * C + a) // 16 : (e * C + b) // 16]
+            nc.vector.tensor_copy(gw[e][:, a:b], xw[:].indirect(lst))
+            nc.vector.tensor_copy(gs[e][:, a:b], xs[:].indirect(lst))
+
+        def first(u):
+            e, a, b = UNITS[u]
+            n = 512 // (b - a)
             for t in range(4):
                 nc.tensor.matmul_mx(
-                    out=a_ps[e][t // 2][:, t % 2, :],
-                    lhsT=w1[e][:, 256 * t : 256 * (t + 1)].bitcast(FP4X4),
-                    lhsT_scale=s1[e][:, P * t : P * (t + 1)],
-                    rhs=gw[e][:].bitcast(FP8X4),
-                    rhs_scale=gs[e][:],
+                    out=a_ps[u][t // n][:, t % n, :],
+                    lhsT=w1[:, e, 256 * t : 256 * (t + 1)].bitcast(FP4X4),
+                    lhsT_scale=s1[:, e, P * t : P * (t + 1)],
+                    rhs=gw[e][:, a:b].bitcast(FP8X4),
+                    rhs_scale=gs[e][:, a:b],
                     start=True,
                     stop=True,
                 )
-        for e in range(E):
-            for b in range(2):
-                nc.scalar.activation(r[e][:, 2 * b : 2 * b + 2, :], a_ps[e][b][:], RELU)
-            half = C // 2
-            for s in range(2):
-                cols = slice(s * half, (s + 1) * half)
-                src = r[e][:, :, cols].rearrange("p t s -> p s t")
-                if e == 0 and s == 1:
-                    nc.vector.tensor_tensor(h_grp[e][:, cols, :], src, src, MULT)
-                else:
-                    nc.scalar.activation(h_grp[e][:, cols, :], src, SQUARE)
+
+        def hidden(u):
+            e, a, b = UNITS[u]
+            n = 512 // (b - a)
+            for i, bank in enumerate(a_ps[u]):
+                nc.scalar.activation(r[u][:, i * n : (i + 1) * n, :], bank[:], RELU)
+            for c in range(0, b - a, 128):
+                nc.scalar.activation(
+                    h_grp[u][:, c : c + 128, :], r[u][:, :, c : c + 128].rearrange("p t s -> p s t"), SQUARE
+                )
             nc.vector.quantize_mx(
-                out=hw[e][:].bitcast(FP8X4), scales=hs[e][:], in_=h_grp[e][:].rearrange("p s t -> p (s t)")
+                out=hw[u][:].bitcast(FP8X4), scales=hs[u][:], in_=h_grp[u][:].rearrange("p s t -> p (s t)")
             )
-            for b in range(4):
+
+        def second(u):
+            e, a, b = UNITS[u]
+            n = 512 // (b - a)
+            for i in range(4):
                 nc.tensor.matmul_mx(
-                    out=y_ps[e][b // 2][:, b % 2, :],
-                    lhsT=w2[e][:, 256 * b : 256 * (b + 1)].bitcast(FP4X4),
-                    lhsT_scale=s2[:, e, P * b : P * (b + 1)],
-                    rhs=hw[e][:].bitcast(FP8X4),
-                    rhs_scale=hs[e][:],
+                    out=y_ps[u][i // n][:, i % n, :],
+                    lhsT=w2[:, e, 256 * i : 256 * (i + 1)].bitcast(FP4X4),
+                    lhsT_scale=s2[:, e, P * i : P * (i + 1)],
+                    rhs=hw[u][:].bitcast(FP8X4),
+                    rhs_scale=hs[u][:],
                     start=True,
                     stop=True,
                 )
-            for b in range(4):
-                if b % 2 == 0:
-                    nc.vector.tensor_tensor(
-                        y_sb[e][b // 2][:],
-                        y_ps[e][b // 2][:],
-                        gate_t[:, e * C : (e + 1) * C].unsqueeze(1).to_broadcast([P, 2, C]),
-                        MULT,
-                    )
-                nc.vector.tensor_copy(
-                    win[b][:].indirect(dst_t[:, e * (C // 16) : (e + 1) * (C // 16)]), y_sb[e][b // 2][:, b % 2, :]
-                )
-                if e == E - 1:
-                    nc.sync.dma_start(out[b * P : (b + 1) * P, :], win[b][:])
+            if u == 0:
+                nc.scalar.copy(y_sb[u][:, 0, :], y_ps[u][0][:, 0, :])
+                nc.scalar.copy(y_sb[u][:, 1:4, :], y_ps[u][0][:, 1:4, :])
+            else:
+                for i, bank in enumerate(y_ps[u]):
+                    nc.scalar.copy(y_sb[u][:, i * n : (i + 1) * n, :], bank[:])
+
+        def scatter(u, i):
+            e, a, b = UNITS[u]
+            nc.vector.tensor_tensor(
+                win[i][:].indirect(dst_t[:, (e * C + a) // 16 : (e * C + b) // 16]),
+                y_sb[u][:, i, :],
+                gate_t[:, e * C + a : e * C + b],
+                MULT,
+            )
+            if u == len(UNITS) - 1:
+                nc.sync.dma_start(out[i * P : (i + 1) * P, :], win[i][:])
+
+        gather(0)
+        first(0)
+        gather(1)
+        first(1)
+        hidden(0)
+        second(0)
+        gather(2)
+        permute(1)
+        scatter(0, 0)
+        hidden(1)
+        second(1)
+        first(2)
+        for i in range(1, 4):
+            scatter(0, i)
+        hidden(2)
+        second(2)
+        for u in (1, 2):
+            for i in range(4):
+                scatter(u, i)

@@ -16,7 +16,7 @@ SQUARE = mybir.ActivationFunctionType.Square
 
 P = 128
 K, T, E, C, H, N = 512, 512, 2, 256, 512, 512
-X0 = 384
+X_CHUNKS = ((0, 256), (256, 384), (384, 512))
 UNITS = ((0, 0, 128), (0, 128, 256), (1, 0, 256))
 FLOPS = 2 * E * C * H * (K + N)
 
@@ -36,33 +36,34 @@ def tile_moe_two_mlp_relu2_kernel(tc, xT, w1_words, w1_scales, w2_words, w2_scal
         warm = keep.tile([P, 1], F32, name="warm")
         w1_raw = keep.tile([P, E, 2 * H], U8, name="w1_raw", align_bytes=64)
         w2 = keep.tile([P, E, 2 * N], U8, name="w2", align_bytes=64)
-        x_raw = [keep.tile([P, 4, w], F32, name=f"x_raw{w}", align_bytes=64) for w in (X0, T - X0)]
+        x_raw = [keep.tile([P, 4, b - a], F32, name=f"x_raw{a}", align_bytes=64) for a, b in X_CHUNKS]
         gate_t = keep.tile([P, E * C], F32, name="gate_t")
 
         nc.vector.memset(s1_raw[:].rearrange("p e i -> p (e i)").bitcast(I32), 0)
-        nc.gpsimd.memset(xs[:], 0)
         nc.vector.memset(s2[:].rearrange("p e i -> p (e i)").bitcast(I32), 0)
         nc.vector.memset(warm[:], 0.0)
         nc.scalar.activation(warm[:], warm[:], SQUARE)
 
         x_rows = xT.rearrange("(p j) w -> p j w", j=4)
         nc.sync.dma_start(offs_t[:], offs)
-        nc.sync.dma_start(w1_raw[:].bitcast(I32), w1_words[:, 0].rearrange("e p b -> p e b").bitcast(I32))
-        nc.sync.dma_start(x_raw[0][:], x_rows[:, :, 0:X0])
-        nc.sync.dma_start(x_raw[1][:], x_rows[:, :, X0:T])
+        nc.sync.dma_start(w1_raw[:, 0, :].bitcast(I32), w1_words[0, 0].bitcast(I32))
+        for i, (a, b) in enumerate(X_CHUNKS):
+            nc.sync.dma_start(x_raw[i][:], x_rows[:, :, a:b])
         for q in range(4):
-            nc.scalar.dma_start(
+            (nc.gpsimd if q == 3 else nc.scalar).dma_start(
                 s1_raw[32 * q : 32 * q + 4].bitcast(I32),
                 w1_scales[:, 0, 4 * q : 4 * q + 4, :].rearrange("e q i -> q e i").bitcast(I32),
             )
-        nc.sync.dma_start(w2[:].bitcast(I32), w2_words[:, 0].rearrange("e p b -> p e b").bitcast(I32))
-        nc.sync.dma_start(dst_t[:], dst)
-        nc.sync.dma_start(gate_t[:], gate[0:P, :])
+        nc.gpsimd.memset(xs[:], 0)
+        nc.sync.dma_start(w1_raw[:, 1, :].bitcast(I32), w1_words[1, 0].bitcast(I32))
         for q in range(4):
-            nc.gpsimd.dma_start(
+            nc.sync.dma_start(
                 s2[32 * q : 32 * q + 4].bitcast(I32),
                 w2_scales[:, 0, 4 * q : 4 * q + 4, :].rearrange("e q i -> q e i").bitcast(I32),
             )
+        nc.sync.dma_start(w2[:].bitcast(I32), w2_words[:, 0].rearrange("e p b -> p e b").bitcast(I32))
+        nc.sync.dma_start(gate_t[:], gate[0:P, :])
+        nc.sync.dma_start(dst_t[:], dst)
 
         w1 = keep.tile([P, E, 2 * H], U8, name="w1", align_bytes=64)
         s1 = keep.tile([P, E, H], U8, name="s1", align_bytes=64)
@@ -79,38 +80,43 @@ def tile_moe_two_mlp_relu2_kernel(tc, xT, w1_words, w1_scales, w2_words, w2_scal
 
         permute(0)
 
-        x_grp = [keep.tile([P, w, 4], BF16, name=f"x_grp{w}", align_bytes=64) for w in (X0, T - X0)]
+        x_grp = keep.tile([P, T, 4], BF16, name="x_grp", align_bytes=64)
 
         def group(i, a, b, engine):
-            src = x_raw[i][:, :, a:b].rearrange("p j w -> p w j")
+            c0 = X_CHUNKS[i][0]
+            src = x_raw[i][:, :, a - c0 : b - c0].rearrange("p j w -> p w j")
             if engine == "s":
-                nc.scalar.copy(x_grp[i][:, a:b, :], src)
+                nc.scalar.copy(x_grp[:, a:b, :], src)
             else:
-                nc.vector.tensor_copy(x_grp[i][:, a:b, :], src)
+                nc.vector.tensor_copy(x_grp[:, a:b, :], src)
 
-        def quantize_x(i, a, b):
-            cols = slice(i * X0 + a, i * X0 + b)
+        def quantize_x(a, b):
             nc.vector.quantize_mx(
-                out=xw[:, cols].bitcast(FP8X4),
-                scales=xs[:, cols],
-                in_=x_grp[i][:, a:b, :].rearrange("p w j -> p (w j)"),
+                out=xw[:, a:b].bitcast(FP8X4),
+                scales=xs[:, a:b],
+                in_=x_grp[:, a:b, :].rearrange("p w j -> p (w j)"),
             )
 
-        group(0, 0, 256, "s")
-        group(0, 256, 384, "v")
-        quantize_x(0, 256, 384)
-        group(1, 0, 64, "s")
-        group(1, 64, 128, "v")
-        quantize_x(0, 0, 256)
-        quantize_x(1, 0, 128)
+        group(0, 0, 128, "v")
+        group(0, 128, 256, "s")
+        group(1, 256, 320, "s")
+        group(1, 320, 384, "v")
+        quantize_x(0, 256)
+        group(2, 384, 432, "s")
+        group(2, 432, 512, "v")
+        quantize_x(256, 384)
+        quantize_x(384, 512)
 
         gw = [keep.tile([P, C], U32, name=f"gw{e}", align_bytes=64) for e in range(E)]
         gs = [keep.tile([P, C], U8, name=f"gs{e}", align_bytes=64) for e in range(E)]
         a_ps, y_ps, r, h_grp, hw, hs, y_sb = [], [], [], [], [], [], []
+        banks = [psum.tile([P, 512], F32, name=f"bank{i}") for i in range(4)]
+        a_banks = ((0,), (0,), (0, 1))
+        y_banks = ((1,), (1,), (2, 3))
         for u, (e, a, b) in enumerate(UNITS):
             w = b - a
-            a_ps.append([psum.tile([P, 512 // w, w], F32, name=f"a_ps{u}_{i}") for i in range(4 * w // 512)])
-            y_ps.append([psum.tile([P, 512 // w, w], F32, name=f"y_ps{u}_{i}") for i in range(4 * w // 512)])
+            a_ps.append([banks[i][:].rearrange("p (t s) -> p t s", s=w) for i in a_banks[u]])
+            y_ps.append([banks[i][:].rearrange("p (t s) -> p t s", s=w) for i in y_banks[u]])
             r.append(keep.tile([P, 4, w], F32, name=f"r{u}", align_bytes=64))
             h_grp.append(keep.tile([P, w, 4], BF16, name=f"h_grp{u}", align_bytes=64))
             hw.append(keep.tile([P, w], U32, name=f"hw{u}", align_bytes=64))
@@ -142,7 +148,7 @@ def tile_moe_two_mlp_relu2_kernel(tc, xT, w1_words, w1_scales, w2_words, w2_scal
             e, a, b = UNITS[u]
             n = 512 // (b - a)
             for i, bank in enumerate(a_ps[u]):
-                nc.scalar.activation(r[u][:, i * n : (i + 1) * n, :], bank[:], RELU)
+                nc.scalar.activation(r[u][:, i * n : (i + 1) * n, :], bank, RELU)
             for c in range(0, b - a, 128):
                 nc.scalar.activation(
                     h_grp[u][:, c : c + 128, :], r[u][:, :, c : c + 128].rearrange("p t s -> p s t"), SQUARE
@@ -169,7 +175,7 @@ def tile_moe_two_mlp_relu2_kernel(tc, xT, w1_words, w1_scales, w2_words, w2_scal
                 nc.scalar.copy(y_sb[u][:, 1:4, :], y_ps[u][0][:, 1:4, :])
             else:
                 for i, bank in enumerate(y_ps[u]):
-                    nc.scalar.copy(y_sb[u][:, i * n : (i + 1) * n, :], bank[:])
+                    nc.scalar.copy(y_sb[u][:, i * n : (i + 1) * n, :], bank)
 
         def scatter(u, i):
             e, a, b = UNITS[u]
@@ -184,20 +190,21 @@ def tile_moe_two_mlp_relu2_kernel(tc, xT, w1_words, w1_scales, w2_words, w2_scal
 
         gather(0)
         first(0)
+        hidden(0)
         gather(1)
         first(1)
-        hidden(0)
         second(0)
         gather(2)
         permute(1)
         scatter(0, 0)
         hidden(1)
-        second(1)
         first(2)
+        hidden(2)
         for i in range(1, 4):
             scatter(0, i)
-        hidden(2)
+        second(1)
+        for i in range(4):
+            scatter(1, i)
         second(2)
-        for u in (1, 2):
-            for i in range(4):
-                scatter(u, i)
+        for i in range(4):
+            scatter(2, i)

@@ -18,6 +18,7 @@ P = 128
 K, T, E, C, H, N = 512, 512, 2, 256, 512, 512
 X_CHUNKS = ((0, 256), (256, 384), (384, 512))
 UNITS = ((0, 0, 128), (0, 128, 256), (1, 0, 256))
+W0 = 128
 FLOPS = 2 * E * C * H * (K + N)
 
 
@@ -36,7 +37,7 @@ def tile_moe_two_mlp_relu2_kernel(tc, xT, w1_words, w1_scales, w2_words, w2_scal
         warm = keep.tile([P, 1], F32, name="warm")
         w1_raw = keep.tile([P, E, 2 * H], U8, name="w1_raw", align_bytes=64)
         w2 = keep.tile([P, E, 2 * N], U8, name="w2", align_bytes=64)
-        x_raw = [keep.tile([P, 4, b - a], F32, name=f"x_raw{a}", align_bytes=64) for a, b in X_CHUNKS]
+        x_raw = [keep.tile([P, 4, b - a], F32, name=f"x_raw{a}", tag=f"slot{a}", align_bytes=64) for a, b in X_CHUNKS]
         gate_t = keep.tile([P, E * C], F32, name="gate_t")
 
         nc.vector.memset(s1_raw[:].rearrange("p e i -> p (e i)").bitcast(I32), 0)
@@ -45,15 +46,15 @@ def tile_moe_two_mlp_relu2_kernel(tc, xT, w1_words, w1_scales, w2_words, w2_scal
         nc.scalar.activation(warm[:], warm[:], SQUARE)
 
         x_rows = xT.rearrange("(p j) w -> p j w", j=4)
-        nc.sync.dma_start(offs_t[:], offs)
-        nc.sync.dma_start(w1_raw[:, 0, :].bitcast(I32), w1_words[0, 0].bitcast(I32))
-        for i, (a, b) in enumerate(X_CHUNKS):
-            nc.sync.dma_start(x_raw[i][:], x_rows[:, :, a:b])
         for q in range(4):
             (nc.gpsimd if q == 3 else nc.scalar).dma_start(
                 s1_raw[32 * q : 32 * q + 4].bitcast(I32),
                 w1_scales[:, 0, 4 * q : 4 * q + 4, :].rearrange("e q i -> q e i").bitcast(I32),
             )
+        nc.sync.dma_start(offs_t[:], offs)
+        nc.sync.dma_start(w1_raw[:, 0, :].bitcast(I32), w1_words[0, 0].bitcast(I32))
+        for i, (a, b) in enumerate(X_CHUNKS):
+            nc.sync.dma_start(x_raw[i][:], x_rows[:, :, a:b])
         nc.gpsimd.memset(xs[:], 0)
         nc.sync.dma_start(w1_raw[:, 1, :].bitcast(I32), w1_words[1, 0].bitcast(I32))
         for q in range(4):
@@ -65,53 +66,56 @@ def tile_moe_two_mlp_relu2_kernel(tc, xT, w1_words, w1_scales, w2_words, w2_scal
         nc.sync.dma_start(gate_t[:], gate[0:P, :])
         nc.sync.dma_start(dst_t[:], dst)
 
-        w1 = keep.tile([P, E, 2 * H], U8, name="w1", align_bytes=64)
-        s1 = keep.tile([P, E, H], U8, name="s1", align_bytes=64)
-
-        def permute(e):
+        def permute_words(e, dest):
             nc.vector.tensor_copy(
-                w1[:, e, :].bitcast(U16).rearrange("p (t m) -> p t m", t=4),
+                dest[:].bitcast(U16).rearrange("p (t m) -> p t m", t=4),
                 w1_raw[:, e, :].bitcast(U16).rearrange("p (m t) -> p t m", t=4),
             )
+
+        def permute_scales(e, dest):
             nc.vector.tensor_copy(
-                s1[:, e, :].rearrange("p (t m) -> p t m", t=4),
+                dest[:].rearrange("p (t m) -> p t m", t=4),
                 s1_raw[:, e, :].rearrange("p (m t) -> p t m", t=4),
             )
 
-        permute(0)
+        w1 = [keep.tile([P, 2 * H], U8, name="w1_0", align_bytes=64)]
+        permute_words(0, w1[0])
 
-        x_grp = keep.tile([P, T, 4], BF16, name="x_grp", align_bytes=64)
+        x_grp = [keep.tile([P, 256, 4], BF16, name=f"x_grp{i}", tag=f"grp{i}", align_bytes=64) for i in range(2)]
 
         def group(i, a, b, engine):
             c0 = X_CHUNKS[i][0]
             src = x_raw[i][:, :, a - c0 : b - c0].rearrange("p j w -> p w j")
+            dest = x_grp[a // 256][:, a % 256 : (b - 1) % 256 + 1, :]
             if engine == "s":
-                nc.scalar.copy(x_grp[:, a:b, :], src)
+                nc.scalar.copy(dest, src)
             else:
-                nc.vector.tensor_copy(x_grp[:, a:b, :], src)
+                nc.vector.tensor_copy(dest, src)
 
-        def quantize_x(a, b):
+        def quantize_x(i):
+            cols = slice(256 * i, 256 * (i + 1))
             nc.vector.quantize_mx(
-                out=xw[:, a:b].bitcast(FP8X4),
-                scales=xs[:, a:b],
-                in_=x_grp[:, a:b, :].rearrange("p w j -> p (w j)"),
+                out=xw[:, cols].bitcast(FP8X4), scales=xs[:, cols], in_=x_grp[i][:].rearrange("p w j -> p (w j)")
             )
 
-        group(0, 0, 128, "v")
-        group(0, 128, 256, "s")
-        group(1, 256, 320, "s")
-        group(1, 320, 384, "v")
-        quantize_x(0, 256)
+        group(0, 0, 160, "v")
+        group(0, 160, 256, "s")
+        quantize_x(0)
+        group(1, 256, 336, "s")
+        group(1, 336, 384, "v")
         group(2, 384, 432, "s")
         group(2, 432, 512, "v")
-        quantize_x(256, 384)
-        quantize_x(384, 512)
+        quantize_x(1)
+        s1 = [keep.tile([P, H], U8, name="s1_0", tag="grp0", align_bytes=64)]
+        permute_scales(0, s1[0])
 
         gw = [keep.tile([P, C], U32, name=f"gw{e}", align_bytes=64) for e in range(E)]
         gs = [keep.tile([P, C], U8, name=f"gs{e}", align_bytes=64) for e in range(E)]
         a_ps, y_ps, r, h_grp, hw, hs, y_sb = [], [], [], [], [], [], []
-        banks = [psum.tile([P, 512], F32, name=f"bank{i}") for i in range(4)]
+        banks = [psum.tile([P, 512], F32, name=f"bank{i}") for i in range(6)]
         a_banks = ((0,), (0,), (0, 1))
+        a_hi = banks[4][:].rearrange("p (t s) -> p t s", s=W0)
+        y_first = banks[5][:].rearrange("p (t s) -> p t s", s=W0)
         y_banks = ((1,), (1,), (2, 3))
         for u, (e, a, b) in enumerate(UNITS):
             w = b - a
@@ -135,9 +139,9 @@ def tile_moe_two_mlp_relu2_kernel(tc, xT, w1_words, w1_scales, w2_words, w2_scal
             n = 512 // (b - a)
             for t in range(4):
                 nc.tensor.matmul_mx(
-                    out=a_ps[u][t // n][:, t % n, :],
-                    lhsT=w1[:, e, 256 * t : 256 * (t + 1)].bitcast(FP4X4),
-                    lhsT_scale=s1[:, e, P * t : P * (t + 1)],
+                    out=(a_hi if u == 0 and t >= 2 else a_ps[u][t // n])[:, t % n, :],
+                    lhsT=w1[e][:, 256 * t : 256 * (t + 1)].bitcast(FP4X4),
+                    lhsT_scale=s1[e][:, P * t : P * (t + 1)],
                     rhs=gw[e][:, a:b].bitcast(FP8X4),
                     rhs_scale=gs[e][:, a:b],
                     start=True,
@@ -147,8 +151,12 @@ def tile_moe_two_mlp_relu2_kernel(tc, xT, w1_words, w1_scales, w2_words, w2_scal
         def hidden(u):
             e, a, b = UNITS[u]
             n = 512 // (b - a)
-            for i, bank in enumerate(a_ps[u]):
-                nc.scalar.activation(r[u][:, i * n : (i + 1) * n, :], bank, RELU)
+            if u == 0:
+                nc.scalar.activation(r[u][:, 0:2, :], a_ps[u][0][:, 0:2, :], RELU)
+                nc.scalar.activation(r[u][:, 2:4, :], a_hi[:, 2:4, :], RELU)
+            else:
+                for i, bank in enumerate(a_ps[u]):
+                    nc.scalar.activation(r[u][:, i * n : (i + 1) * n, :], bank, RELU)
             for c in range(0, b - a, 128):
                 nc.scalar.activation(
                     h_grp[u][:, c : c + 128, :], r[u][:, :, c : c + 128].rearrange("p t s -> p s t"), SQUARE
@@ -162,7 +170,7 @@ def tile_moe_two_mlp_relu2_kernel(tc, xT, w1_words, w1_scales, w2_words, w2_scal
             n = 512 // (b - a)
             for i in range(4):
                 nc.tensor.matmul_mx(
-                    out=y_ps[u][i // n][:, i % n, :],
+                    out=(y_first if u == 0 and i == 0 else y_ps[u][i // n])[:, i % n, :],
                     lhsT=w2[:, e, 256 * i : 256 * (i + 1)].bitcast(FP4X4),
                     lhsT_scale=s2[:, e, P * i : P * (i + 1)],
                     rhs=hw[u][:].bitcast(FP8X4),
@@ -171,7 +179,7 @@ def tile_moe_two_mlp_relu2_kernel(tc, xT, w1_words, w1_scales, w2_words, w2_scal
                     stop=True,
                 )
             if u == 0:
-                nc.scalar.copy(y_sb[u][:, 0, :], y_ps[u][0][:, 0, :])
+                nc.scalar.copy(y_sb[u][:, 0, :], y_first[:, 0, :])
                 nc.scalar.copy(y_sb[u][:, 1:4, :], y_ps[u][0][:, 1:4, :])
             else:
                 for i, bank in enumerate(y_ps[u]):
@@ -195,7 +203,10 @@ def tile_moe_two_mlp_relu2_kernel(tc, xT, w1_words, w1_scales, w2_words, w2_scal
         first(1)
         second(0)
         gather(2)
-        permute(1)
+        w1.append(keep.tile([P, 2 * H], U8, name="w1_1", tag="grp1", align_bytes=64))
+        s1.append(keep.tile([P, H], U8, name="s1_1", tag="slot384", align_bytes=64))
+        permute_words(1, w1[1])
+        permute_scales(1, s1[1])
         scatter(0, 0)
         hidden(1)
         first(2)

@@ -16,7 +16,7 @@ SQUARE = mybir.ActivationFunctionType.Square
 
 P = 128
 K, T, E, C, H, N = 512, 512, 2, 256, 512, 512
-X_CHUNKS = ((0, 256), (256, 384), (384, 512))
+X_CHUNKS = ((0, 384), (384, 512))
 UNITS = ((0, 0, 128), (0, 128, 256), (1, 0, 256))
 W0 = 128
 FLOPS = 2 * E * C * H * (K + N)
@@ -47,7 +47,7 @@ def tile_moe_two_mlp_relu2_kernel(tc, xT, w1_words, w1_scales, w2_words, w2_scal
 
         x_rows = xT.rearrange("(p j) w -> p j w", j=4)
         for q in range(4):
-            (nc.gpsimd if q == 3 else nc.scalar).dma_start(
+            nc.scalar.dma_start(
                 s1_raw[32 * q : 32 * q + 4].bitcast(I32),
                 w1_scales[:, 0, 4 * q : 4 * q + 4, :].rearrange("e q i -> q e i").bitcast(I32),
             )
@@ -98,13 +98,13 @@ def tile_moe_two_mlp_relu2_kernel(tc, xT, w1_words, w1_scales, w2_words, w2_scal
                 out=xw[:, cols].bitcast(FP8X4), scales=xs[:, cols], in_=x_grp[i][:].rearrange("p w j -> p (w j)")
             )
 
-        group(0, 0, 160, "v")
-        group(0, 160, 256, "s")
+        group(0, 0, 176, "v")
+        group(0, 176, 256, "s")
         quantize_x(0)
-        group(1, 256, 336, "s")
-        group(1, 336, 384, "v")
-        group(2, 384, 432, "s")
-        group(2, 432, 512, "v")
+        group(0, 256, 320, "s")
+        group(0, 320, 384, "v")
+        group(1, 384, 432, "s")
+        group(1, 432, 512, "v")
         quantize_x(1)
         s1 = [keep.tile([P, H], U8, name="s1_0", tag="grp0", align_bytes=64)]
         permute_scales(0, s1[0])

from contextlib import ExitStack

import concourse.mybir as mybir

F32 = mybir.dt.float32
BF16 = mybir.dt.bfloat16
I32 = mybir.dt.int32
U32 = mybir.dt.uint32
U16 = mybir.dt.uint16
U8 = mybir.dt.uint8
FP8X4 = mybir.dt.float8_e4m3fn_x4
FP4X4 = mybir.dt.float4_e2m1fn_x4
MULT = mybir.AluOpType.mult
RELU = mybir.ActivationFunctionType.Relu
SQUARE = mybir.ActivationFunctionType.Square

P = 128
K, T, E, C, H, N = 512, 512, 2, 256, 512, 512
X_CHUNKS = ((0, 384), (384, 512))
UNITS = ((0, 0, 128), (0, 128, 256), (1, 0, 256))
W0 = 128
FLOPS = 2 * E * C * H * (K + N)


def tile_moe_two_mlp_relu2_kernel(tc, xT, w1_words, w1_scales, w2_words, w2_scales, gate, offs, dst, out):
    nc = tc.nc
    with ExitStack() as ctx:
        keep = ctx.enter_context(tc.tile_pool(name="keep", bufs=1))
        psum = ctx.enter_context(tc.psum_pool(name="psum", bufs=1))

        offs_t = keep.tile([P, T // 16], U16, name="offs_t")
        dst_t = keep.tile([P, T // 16], U16, name="dst_t")
        s1_raw = keep.tile([P, E, H], U8, name="s1_raw", align_bytes=64)
        s2 = keep.tile([P, E, N], U8, name="s2", align_bytes=64)
        xs = keep.tile([P, T], U8, name="xs", align_bytes=64)
        xw = keep.tile([P, T], U32, name="xw", align_bytes=64)
        warm = keep.tile([P, 1], F32, name="warm")
        w1_raw = keep.tile([P, E, 2 * H], U8, name="w1_raw", align_bytes=64)
        w2 = keep.tile([P, E, 2 * N], U8, name="w2", align_bytes=64)
        x_raw = [keep.tile([P, 4, b - a], F32, name=f"x_raw{a}", tag=f"slot{a}", align_bytes=64) for a, b in X_CHUNKS]
        gate_t = keep.tile([P, E * C], F32, name="gate_t")

        nc.vector.memset(s1_raw[:].rearrange("p e i -> p (e i)").bitcast(I32), 0)
        nc.vector.memset(s2[:].rearrange("p e i -> p (e i)").bitcast(I32), 0)
        nc.vector.memset(warm[:], 0.0)
        nc.scalar.activation(warm[:], warm[:], SQUARE)

        x_rows = xT.rearrange("(p j) w -> p j w", j=4)
        for q in range(4):
            nc.scalar.dma_start(
                s1_raw[32 * q : 32 * q + 4].bitcast(I32),
                w1_scales[:, 0, 4 * q : 4 * q + 4, :].rearrange("e q i -> q e i").bitcast(I32),
            )
        nc.sync.dma_start(offs_t[:], offs)
        nc.sync.dma_start(w1_raw[:, 0, :].bitcast(I32), w1_words[0, 0].bitcast(I32))
        for i, (a, b) in enumerate(X_CHUNKS):
            nc.sync.dma_start(x_raw[i][:], x_rows[:, :, a:b])
        nc.gpsimd.memset(xs[:], 0)
        nc.sync.dma_start(w1_raw[:, 1, :].bitcast(I32), w1_words[1, 0].bitcast(I32))
        for q in range(4):
            nc.sync.dma_start(
                s2[32 * q : 32 * q + 4].bitcast(I32),
                w2_scales[:, 0, 4 * q : 4 * q + 4, :].rearrange("e q i -> q e i").bitcast(I32),
            )
        nc.sync.dma_start(w2[:].bitcast(I32), w2_words[:, 0].rearrange("e p b -> p e b").bitcast(I32))
        nc.sync.dma_start(gate_t[:], gate[0:P, :])
        nc.sync.dma_start(dst_t[:], dst)

        def permute_words(e, dest):
            nc.vector.tensor_copy(
                dest[:].bitcast(U16).rearrange("p (t m) -> p t m", t=4),
                w1_raw[:, e, :].bitcast(U16).rearrange("p (m t) -> p t m", t=4),
            )

        def permute_scales(e, dest):
            nc.vector.tensor_copy(
                dest[:].rearrange("p (t m) -> p t m", t=4),
                s1_raw[:, e, :].rearrange("p (m t) -> p t m", t=4),
            )

        w1 = [keep.tile([P, 2 * H], U8, name="w1_0", align_bytes=64)]
        permute_words(0, w1[0])

        x_grp = [keep.tile([P, 256, 4], BF16, name=f"x_grp{i}", tag=f"grp{i}", align_bytes=64) for i in range(2)]

        def group(i, a, b, engine):
            c0 = X_CHUNKS[i][0]
            src = x_raw[i][:, :, a - c0 : b - c0].rearrange("p j w -> p w j")
            dest = x_grp[a // 256][:, a % 256 : (b - 1) % 256 + 1, :]
            if engine == "s":
                nc.scalar.copy(dest, src)
            else:
                nc.vector.tensor_copy(dest, src)

        def quantize_x(i):
            cols = slice(256 * i, 256 * (i + 1))
            nc.vector.quantize_mx(
                out=xw[:, cols].bitcast(FP8X4), scales=xs[:, cols], in_=x_grp[i][:].rearrange("p w j -> p (w j)")
            )

        group(0, 0, 176, "v")
        group(0, 176, 256, "s")
        quantize_x(0)
        group(0, 256, 320, "s")
        group(0, 320, 384, "v")
        group(1, 384, 432, "s")
        group(1, 432, 512, "v")
        quantize_x(1)
        s1 = [keep.tile([P, H], U8, name="s1_0", tag="grp0", align_bytes=64)]
        permute_scales(0, s1[0])

        gw = [keep.tile([P, C], U32, name=f"gw{e}", align_bytes=64) for e in range(E)]
        gs = [keep.tile([P, C], U8, name=f"gs{e}", align_bytes=64) for e in range(E)]
        a_ps, y_ps, r, h_grp, hw, hs, y_sb = [], [], [], [], [], [], []
        banks = [psum.tile([P, 512], F32, name=f"bank{i}") for i in range(6)]
        a_banks = ((0,), (0,), (0, 1))
        a_hi = banks[4][:].rearrange("p (t s) -> p t s", s=W0)
        y_first = banks[5][:].rearrange("p (t s) -> p t s", s=W0)
        y_banks = ((1,), (1,), (2, 3))
        for u, (e, a, b) in enumerate(UNITS):
            w = b - a
            a_ps.append([banks[i][:].rearrange("p (t s) -> p t s", s=w) for i in a_banks[u]])
            y_ps.append([banks[i][:].rearrange("p (t s) -> p t s", s=w) for i in y_banks[u]])
            r.append(keep.tile([P, 4, w], F32, name=f"r{u}", align_bytes=64))
            h_grp.append(keep.tile([P, w, 4], BF16, name=f"h_grp{u}", align_bytes=64))
            hw.append(keep.tile([P, w], U32, name=f"hw{u}", align_bytes=64))
            hs.append(keep.tile([P, w], U8, name=f"hs{u}", align_bytes=64))
            y_sb.append(keep.tile([P, 4, w], F32, name=f"y_sb{u}"))
        win = [keep.tile([P, T], F32, name=f"win{b}") for b in range(4)]

        def gather(u):
            e, a, b = UNITS[u]
            lst = offs_t[:, (e * C + a) // 16 : (e * C + b) // 16]
            nc.vector.tensor_copy(gw[e][:, a:b], xw[:].indirect(lst))
            nc.vector.tensor_copy(gs[e][:, a:b], xs[:].indirect(lst))

        def first(u):
            e, a, b = UNITS[u]
            n = 512 // (b - a)
            for t in range(4):
                nc.tensor.matmul_mx(
                    out=(a_hi if u == 0 and t >= 2 else a_ps[u][t // n])[:, t % n, :],
                    lhsT=w1[e][:, 256 * t : 256 * (t + 1)].bitcast(FP4X4),
                    lhsT_scale=s1[e][:, P * t : P * (t + 1)],
                    rhs=gw[e][:, a:b].bitcast(FP8X4),
                    rhs_scale=gs[e][:, a:b],
                    start=True,
                    stop=True,
                )

        def hidden(u):
            e, a, b = UNITS[u]
            n = 512 // (b - a)
            if u == 0:
                nc.scalar.activation(r[u][:, 0:2, :], a_ps[u][0][:, 0:2, :], RELU)
                nc.scalar.activation(r[u][:, 2:4, :], a_hi[:, 2:4, :], RELU)
            else:
                for i, bank in enumerate(a_ps[u]):
                    nc.scalar.activation(r[u][:, i * n : (i + 1) * n, :], bank, RELU)
            for c in range(0, b - a, 128):
                nc.scalar.activation(
                    h_grp[u][:, c : c + 128, :], r[u][:, :, c : c + 128].rearrange("p t s -> p s t"), SQUARE
                )
            nc.vector.quantize_mx(
                out=hw[u][:].bitcast(FP8X4), scales=hs[u][:], in_=h_grp[u][:].rearrange("p s t -> p (s t)")
            )

        def second(u):
            e, a, b = UNITS[u]
            n = 512 // (b - a)
            for i in range(4):
                nc.tensor.matmul_mx(
                    out=(y_first if u == 0 and i == 0 else y_ps[u][i // n])[:, i % n, :],
                    lhsT=w2[:, e, 256 * i : 256 * (i + 1)].bitcast(FP4X4),
                    lhsT_scale=s2[:, e, P * i : P * (i + 1)],
                    rhs=hw[u][:].bitcast(FP8X4),
                    rhs_scale=hs[u][:],
                    start=True,
                    stop=True,
                )
            if u == 0:
                nc.scalar.copy(y_sb[u][:, 0, :], y_first[:, 0, :])
                nc.scalar.copy(y_sb[u][:, 1:4, :], y_ps[u][0][:, 1:4, :])
            else:
                for i, bank in enumerate(y_ps[u]):
                    nc.scalar.copy(y_sb[u][:, i * n : (i + 1) * n, :], bank)

        def scatter(u, i):
            e, a, b = UNITS[u]
            nc.vector.tensor_tensor(
                win[i][:].indirect(dst_t[:, (e * C + a) // 16 : (e * C + b) // 16]),
                y_sb[u][:, i, :],
                gate_t[:, e * C + a : e * C + b],
                MULT,
            )
            if u == len(UNITS) - 1:
                nc.sync.dma_start(out[i * P : (i + 1) * P, :], win[i][:])

        gather(0)
        first(0)
        hidden(0)
        gather(1)
        first(1)
        second(0)
        gather(2)
        w1.append(keep.tile([P, 2 * H], U8, name="w1_1", tag="grp1", align_bytes=64))
        s1.append(keep.tile([P, H], U8, name="s1_1", tag="slot384", align_bytes=64))
        permute_words(1, w1[1])
        permute_scales(1, s1[1])
        scatter(0, 0)
        hidden(1)
        first(2)
        hidden(2)
        for i in range(1, 4):
            scatter(0, i)
        second(1)
        for i in range(4):
            scatter(1, i)
        second(2)
        for i in range(4):
            scatter(2, i)
